import numpy as np
import ml_dtypes


def mxq(x, axis, fmt="e4m3"):
    dtype, down = {"e4m3": (ml_dtypes.float8_e4m3fn, 7), "e5m2": (ml_dtypes.float8_e5m2, 14)}[fmt]
    v = np.moveaxis(np.asarray(x, np.float32).astype(ml_dtypes.bfloat16).astype(np.float64), axis, -1)
    blocks = v.reshape(v.shape[:-1] + (-1, 32))
    amax = np.abs(blocks).max(-1, keepdims=True)
    byte = np.maximum(np.where(amax > 0, np.frexp(amax)[1] - 1 + 127, 0) - down, 1)
    scale = np.exp2(byte - 127.0)
    codes = (blocks / scale).astype(np.float32).astype(dtype).astype(np.float64)
    return np.moveaxis((codes * scale).reshape(v.shape), -1, axis)


WIDE = False


def mx_kscale(k):
    if not WIDE:
        return np.ones(k)
    levels = np.array([10, -10, 5, -5, 0])
    if k % 512:
        return np.exp2(np.random.permutation(np.resize(levels, k // 32))).repeat(32)
    a = np.empty((k // 512, 16))
    for p in range(k // 512):
        a[p, :8] = np.random.permutation(np.resize(levels, 8))
        for g in range(8):
            far = levels[np.abs(levels - a[p, g]) >= 10]
            a[p, g + 8] = far[np.random.randint(len(far))]
    return np.exp2(a.ravel()).repeat(32)


BF16 = ml_dtypes.bfloat16


def bf(x):
    return np.asarray(x, np.float32).astype(BF16)


def f64(x):
    return np.asarray(x).astype(np.float64)


E2M1 = np.array([0.0, 0.5, 1.0, 1.5, 2.0, 3.0, 4.0, 6.0, -0.0, -0.5, -1.0, -1.5, -2.0, -3.0, -4.0, -6.0])


def pack_weight(w, fmt):
    k, n = w.shape
    w = f64(bf(w)).reshape(k // 32, 32, n)
    amax = np.abs(w).max(1)
    if fmt == "e4m3":
        byte = np.frexp(amax)[1] - 1 + 127 - 7
    else:
        mant, ex = np.frexp(amax / 6.0)
        byte = np.where(mant > 0.5, ex, ex - 1) + 127
    byte = np.clip(np.where(amax > 0, byte, 1), 1, 254)
    scaled = (w * np.exp2(127.0 - byte)[:, None, :]).reshape(k, n).astype(np.float32)
    by_word = np.ascontiguousarray(scaled.reshape(k // 512, 128, 4, n).transpose(0, 1, 3, 2))
    if fmt == "e4m3":
        words = by_word.astype(ml_dtypes.float8_e4m3fn).view(np.uint8)
    else:
        c = by_word.astype(ml_dtypes.float4_e2m1fn).view(np.uint8) & 0xF
        words = c[..., 0::2] | (c[..., 1::2] << 4)
    return np.ascontiguousarray(words), np.ascontiguousarray(byte.astype(np.uint8).reshape(k // 512, 16, n))


def unpack_weight(words, scales, fmt):
    g, p, n, _ = words.shape
    if fmt == "e4m3":
        vals = np.ascontiguousarray(words).view(ml_dtypes.float8_e4m3fn).astype(np.float64)
    else:
        nib = np.empty((g, p, n, 4), np.uint8)
        nib[..., 0::2] = words & 0xF
        nib[..., 1::2] = words >> 4
        vals = E2M1[nib]
    vals = vals * np.repeat(np.exp2(scales.astype(np.float64) - 127.0), 8, axis=1)[..., None]
    return vals.transpose(0, 1, 3, 2).reshape(g * 512, n)
def pack4(w):
    words, scales = pack_weight(w, "e2m1")
    return words.reshape(words.shape[0], 128, -1), scales


def unpack4(words, scales):
    return unpack_weight(words.reshape(words.shape[0], 128, -1, 2), scales, "e2m1")


M, K, J, P = 1536, 1024, 1024, 512


def setup_inputs():
    s, u, j, t = mx_kscale(K), mx_kscale(M), mx_kscale(J), mx_kscale(P)
    c = 0.5 + np.random.random_sample(P)
    left = np.random.standard_normal((K, M)) * s[:, None]
    right = np.random.standard_normal((K, M)) / np.sqrt(K) / M ** 0.25 / s[:, None] * u
    left_words, left_scales = pack4(left)
    right_words, right_scales = pack4(right)
    return {"left_words": left_words, "left_scales": left_scales,
            "right_words": right_words, "right_scales": right_scales,
            "krylov": bf(np.random.standard_normal((M, J)) * j / u[:, None]),
            "coef": bf(np.random.standard_normal((J, P)) / np.sqrt(J) / M ** 0.25 / j[:, None] * c),
            "bv": bf(np.random.standard_normal((M, P)) * t),
            "proj": bf(np.random.standard_normal((P, P)) / np.sqrt(P) / t[:, None] * c)}


def reference(left_words, left_scales, right_words, right_scales, krylov, coef, bv, proj):
    a = unpack4(left_words, left_scales).T @ unpack4(right_words, right_scales)
    v = mxq(f64(krylov), 1, "e4m3") @ mxq(f64(coef), 0, "e4m3")
    av = mxq(a, 1, "e4m3") @ mxq(v, 0, "e4m3")
    bvt = mxq(f64(bv), 1, "e4m3") @ mxq(f64(proj), 0, "e4m3")
    resid = av - bvt
    sq = np.mean(np.square(resid), axis=0)
    return resid, sq

@@ -1,0 +1,345 @@
+from contextlib import ExitStack
+
+import concourse.mybir as mybir
+from concourse.masks import make_identity
+
+M, K, J, P = 1536, 1024, 1024, 512
+FLOPS = 2 * (M * M * K + M * J * P + M * M * P + M * P * P)
+
+F32 = mybir.dt.float32
+BF16 = mybir.dt.bfloat16
+I32 = mybir.dt.int32
+U32 = mybir.dt.uint32
+U8 = mybir.dt.uint8
+FP8X4 = mybir.dt.float8_e4m3fn_x4
+FP4X4 = mybir.dt.float4_e2m1fn_x4
+ACT = mybir.ActivationFunctionType
+ALU = mybir.AluOpType
+
+PARTS = 128
+PASS = 512
+BANK = 512
+M_PASSES = M // PASS
+K_PASSES = K // PASS
+J_PASSES = J // PASS
+ROW_TILES = M // PARTS
+WARM_UP = 7
+
+
+def tile_ritz_residual_block_s12_kernel(
+    tc, left_words, left_scales, right_words, right_scales, krylov, coef, bv, proj, out_0, out_1
+):
+    nc = tc.nc
+    with ExitStack() as ctx:
+        keep = ctx.enter_context(tc.tile_pool(name="keep", bufs=1))
+        stage = ctx.enter_context(tc.tile_pool(name="stage", bufs=4))
+        psum = ctx.enter_context(tc.psum_pool(name="psum", bufs=8))
+        ctx.enter_context(tc.manual_schedule())
+
+        def kept(name, shape, dtype):
+            return keep.tile(shape, dtype, name=name, align_bytes=64)
+
+        def new_bank():
+            return psum.tile([PARTS, BANK], F32, name="bank")
+
+        def new_grouped():
+            return stage.tile([PARTS, 4 * PASS], BF16, name="grouped", align_bytes=64, bufs=6)
+
+        right_sc_raw = kept("right_sc_raw", [PARTS, K_PASSES, M], U8)
+        left_sc = kept("left_sc", [PARTS, K_PASSES, M], U8)
+        nc.vector.memset(right_sc_raw[:].bitcast(I32), 0)
+        nc.vector.memset(left_sc[:].bitcast(I32), 0)
+        warm = kept("warm", [PARTS, BANK], BF16)
+        nc.gpsimd.memset(warm[:], 0.0)
+        ident = kept("ident", [PARTS, PARTS], F32)
+        make_identity(nc, ident[:])
+        ones = kept("ones", [PARTS, PARTS], F32)
+        nc.gpsimd.memset(ones[:], 1.0)
+        table = kept("table", [PARTS, 1], F32)
+        nc.scalar.activation(out=table[:], in_=warm[:, 0:1], func=ACT.Square)
+        warm_bank = new_bank()
+        for step in range(WARM_UP):
+            nc.tensor.matmul(warm_bank[:], lhsT=warm[:, 0:PARTS], rhs=warm[:], start=True, stop=True)
+
+        def load_words(name, words, c):
+            tile = kept(name + str(c), [PARTS, K_PASSES, 2 * PASS], U8)
+            src = words[:, :, 2 * PASS * c : 2 * PASS * (c + 1)].rearrange("g p b -> p g b")
+            nc.sync.dma_start(out=tile[:].bitcast(I32), in_=src.bitcast(I32))
+            return tile
+
+        def load_scales(plane, scales):
+            rows = scales.bitcast(I32).rearrange("g (Q r) w -> r Q g w", r=4)
+            for r in range(4):
+                nc.sync.dma_start(out=plane[r:PARTS:32, :, :].bitcast(I32), in_=rows[r])
+
+        def load_rows(name, x, first, count):
+            tile = kept(name + str(first), [PARTS, count, x.shape[1]], BF16)
+            src = x[PARTS * first : PARTS * (first + count), :].rearrange("(a p) j -> p a j", p=PARTS)
+            nc.sync.dma_start(out=tile[:], in_=src)
+            return tile
+
+        def load_k_first(name, x, g):
+            tile = kept(name + str(g), [PARTS, 4, P], BF16)
+            nc.sync.dma_start(out=tile[:], in_=x[PASS * g : PASS * (g + 1), :].rearrange("(p t) c -> p t c", t=4))
+            return tile
+
+        right_raw = [load_words("right_raw", right_words, 0)]
+        left = [load_words("left", left_words, 0)]
+        load_scales(right_sc_raw, right_scales)
+        load_scales(left_sc, left_scales)
+        right_raw.append(load_words("right_raw", right_words, 1))
+        right_raw.append(load_words("right_raw", right_words, 2))
+        kry = [load_rows("kry", krylov, 2 * i, 2) for i in range(2)]
+        left.append(load_words("left", left_words, 1))
+        kry.extend([load_rows("kry", krylov, 2 * i, 2) for i in range(2, 6)])
+        coef_raw = [load_k_first("coef_raw", coef, g) for g in range(J_PASSES)]
+        left.append(load_words("left", left_words, 2))
+        bv_raw = [load_rows("bv_raw", bv, 4 * i, 4) for i in range(3)]
+        proj_raw = load_k_first("proj_raw", proj, 0)
+
+        mx = {}
+
+        def quantize(key, grouped):
+            name = "_".join(str(part) for part in key)
+            codes = kept("codes_" + name, [PARTS, PASS], U32)
+            scales = kept("scales_" + name, [PARTS, PASS], U8)
+            nc.vector.quantize_mx(out=codes[:].bitcast(FP8X4), scales=scales[:], in_=grouped[:])
+            mx[key] = (codes, scales)
+
+        def copy_out(on_vector, out, in_):
+            if on_vector:
+                nc.vector.tensor_copy(out=out, in_=in_)
+            else:
+                nc.scalar.copy(out=out, in_=in_)
+
+        right = {}
+
+        def sort_right(G):
+            words = kept("right" + str(G), [PARTS, K_PASSES, 2 * PASS], U8)
+            scales = kept("right_sc" + str(G), [PARTS, K_PASSES, PASS], U8)
+            nc.vector.tensor_copy(
+                out=words[:].bitcast(I32).rearrange("p g (t q w) -> p g t q w", t=4, w=4),
+                in_=right_raw[G][:].bitcast(I32).rearrange("p g (q t w) -> p g t q w", t=4, w=4),
+            )
+            nc.vector.tensor_copy(
+                out=scales[:].bitcast(I32).rearrange("p g (t q w) -> p g t q w", t=4, w=2),
+                in_=right_sc_raw[:, :, PASS * G : PASS * (G + 1)].bitcast(I32).rearrange("p g (q t w) -> p g t q w", t=4, w=2),
+            )
+            right[G] = (words, scales)
+
+        staged = {}
+
+        def interleave(key, raw, negate):
+            grouped = new_grouped()
+            dst = grouped[:].rearrange("p (c i t) -> p c t i", i=4, t=4)
+            src = raw[:].rearrange("p t (c i) -> p c t i", i=4)
+            if negate:
+                nc.vector.tensor_scalar(out=dst, in0=src, scalar1=-1.0, scalar2=None, op0=ALU.mult)
+            else:
+                nc.vector.tensor_copy(out=dst, in_=src)
+            staged[key] = grouped
+
+        def slots_out(on_vector, grouped, b, bank):
+            copy_out(
+                on_vector,
+                grouped[:, BANK * b : BANK * (b + 1)].rearrange("p (n t) -> p n t", t=4),
+                bank[:].rearrange("p (t n) -> p n t", t=4),
+            )
+
+        def a_bank(G, C, b, grouped):
+            words, scales = right[G]
+            bank = new_bank()
+            for t in range(4):
+                for g in range(K_PASSES):
+                    nc.tensor.matmul_mx(
+                        out=bank[:, PARTS * t : PARTS * (t + 1)],
+                        lhsT=words[:, g, 2 * PARTS * t : 2 * PARTS * (t + 1)].bitcast(FP4X4),
+                        lhsT_scale=scales[:, g, PARTS * t : PARTS * (t + 1)],
+                        rhs=left[C][:, g, 2 * PARTS * b : 2 * PARTS * (b + 1)].bitcast(FP4X4),
+                        rhs_scale=left_sc[:, g, PASS * C + PARTS * b : PASS * C + PARTS * (b + 1)],
+                        start=(g == 0),
+                        stop=(g == K_PASSES - 1),
+                    )
+            slots_out(b == 0, grouped, b, bank)
+
+        def v_bank(G, b, grouped):
+            bank = new_bank()
+            for t in range(4):
+                for g in range(J_PASSES):
+                    k_codes, k_scales = mx[("kry", G, g)]
+                    c_codes, c_scales = mx[("coef", g)]
+                    nc.tensor.matmul_mx(
+                        out=bank[:, PARTS * t : PARTS * (t + 1)],
+                        lhsT=k_codes[:, PARTS * t : PARTS * (t + 1)].bitcast(FP8X4),
+                        lhsT_scale=k_scales[:, PARTS * t : PARTS * (t + 1)],
+                        rhs=c_codes[:, PARTS * b : PARTS * (b + 1)].bitcast(FP8X4),
+                        rhs_scale=c_scales[:, PARTS * b : PARTS * (b + 1)],
+                        start=(g == 0),
+                        stop=(g == J_PASSES - 1),
+                    )
+            slots_out(b == 0, grouped, b, bank)
+
+        def turn(words0, words1):
+            bank = new_bank()
+            for u in range(2):
+                for a, words in enumerate((words0, words1)):
+                    col = 2 * PARTS * u + PARTS * a
+                    nc.tensor.transpose(bank[:, col : col + PARTS], words[:, u : 2 * PARTS : 2], ident[:])
+            return bank
+
+        def kry_bank(G, g, half, grouped, on_vector):
+            words = kry[2 * G + half][:].bitcast(F32)
+            bank = turn(words[:, 0, 256 * g : 256 * (g + 1)], words[:, 1, 256 * g : 256 * (g + 1)])
+            dst = grouped[:].bitcast(F32).rearrange("p (t w) -> p t w", t=4)[:, :, PARTS * half : PARTS * (half + 1)]
+            copy_out(on_vector, dst.rearrange("p t (q r u) -> p t q r u", q=8, r=8), bank[:].rearrange("p (u q t r) -> p t q r u", u=2, q=8, t=4))
+
+        def bv_bank(C, half, grouped, on_vector):
+            words = bv_raw[C][:].bitcast(F32)
+            bank = turn(words[:, 2 * half, :], words[:, 2 * half + 1, :])
+            dst = grouped[:].bitcast(F32).rearrange("p (h n u) -> p h n u", h=2, u=2)
+            copy_out(on_vector, dst[:, half], bank[:].rearrange("p (u n) -> p n u", u=2))
+
+        pending = []
+
+        def flush():
+            for job in pending:
+                job()
+            pending.clear()
+
+        def later_quantize(key, grouped):
+            pending.append(lambda: quantize(key, grouped))
+
+        def a_quad(G, C):
+            grouped = new_grouped()
+            for b in range(4):
+                a_bank(G, C, b, grouped)
+                if b == 0:
+                    flush()
+            later_quantize(("a", G, C), grouped)
+
+        def v_quad(G):
+            grouped = new_grouped()
+            for b in range(4):
+                v_bank(G, b, grouped)
+                if b == 0:
+                    flush()
+            later_quantize(("v", G), grouped)
+
+        def kry_quad(G):
+            for g in range(J_PASSES):
+                grouped = new_grouped()
+                for half in range(2):
+                    first = g == 0 and half == 0
+                    kry_bank(G, g, half, grouped, first)
+                    if first:
+                        flush()
+                later_quantize(("kry", G, g), grouped)
+
+        def bv_run(chunks):
+            for C in chunks:
+                grouped = new_grouped()
+                for half in range(2):
+                    first = C == chunks[0] and half == 0
+                    bv_bank(C, half, grouped, first)
+                    if first:
+                        flush()
+                later_quantize(("bv", C), grouped)
+
+        def resid_matmuls(n, cols):
+            C, b = divmod(n, 4)
+            rows = slice(PARTS * b, PARTS * (b + 1))
+            pairs = [(mx[("a", G, C)], mx[("v", G)]) for G in range(M_PASSES)] + [(mx[("bv", C)], mx[("proj",)])]
+            bank = new_bank()
+            for i, (lhs, rhs) in enumerate(pairs):
+                nc.tensor.matmul_mx(
+                    out=bank[:, 0 : cols.stop - cols.start],
+                    lhsT=lhs[0][:, rows].bitcast(FP8X4),
+                    lhsT_scale=lhs[1][:, rows],
+                    rhs=rhs[0][:, cols].bitcast(FP8X4),
+                    rhs_scale=rhs[1][:, cols],
+                    start=(i == 0),
+                    stop=(i == len(pairs) - 1),
+                )
+            return bank
+
+        total = kept("total", [PARTS, P], F32)
+        results = {}
+        squares = {}
+
+        def square(n):
+            if n == 0:
+                nc.scalar.activation(out=total[:], in_=results[n][:], func=ACT.Square)
+            else:
+                sq = stage.tile([PARTS, P], F32, name="sq")
+                nc.scalar.activation(out=sq[:], in_=results[n][:], func=ACT.Square)
+                squares[n] = sq
+
+        def add_square(n):
+            if n > 0:
+                nc.vector.tensor_tensor(out=total[:], in0=total[:], in1=squares[n][:], op=ALU.add)
+
+        def resid_tile(n):
+            bank = resid_matmuls(n, slice(0, P))
+            res = stage.tile([PARTS, P], F32, name="res")
+            copy_out(n % 2 == 0, res[:], bank[:])
+            nc.sync.dma_start(out=out_0[PARTS * n : PARTS * (n + 1), :], in_=res[:])
+            results[n] = res
+            flush()
+            if n >= 1:
+                square(n - 1)
+            if n >= 2:
+                add_square(n - 2)
+
+        sort_right(0)
+        pending.append(lambda: sort_right(1))
+        a_quad(0, 0)
+        pending.append(lambda: sort_right(2))
+        a_quad(1, 0)
+        kry_quad(0)
+        a_quad(2, 0)
+        kry_quad(1)
+        pending.append(lambda: interleave("coef0", coef_raw[0], False))
+        a_quad(0, 1)
+        pending.append(lambda: quantize(("coef", 0), staged["coef0"]))
+        pending.append(lambda: interleave("coef1", coef_raw[1], False))
+        kry_quad(2)
+        pending.append(lambda: quantize(("coef", 1), staged["coef1"]))
+        a_quad(1, 1)
+        pending.append(lambda: interleave("proj", proj_raw, True))
+        v_quad(0)
+        pending.append(lambda: quantize(("proj",), staged["proj"]))
+        bv_run([0, 1])
+        v_quad(1)
+        a_quad(2, 1)
+        bv_run([2])
+        v_quad(2)
+        a_quad(0, 2)
+        a_quad(1, 2)
+        for n in range(4):
+            resid_tile(n)
+        a_quad(2, 2)
+        last = ROW_TILES - 1
+        for n in range(4, last):
+            resid_tile(n)
+
+        half_cols = [slice(0, P // 2), slice(P // 2, P)]
+        banks = [resid_matmuls(last, cols) for cols in half_cols]
+        square(last - 1)
+        add_square(last - 2)
+        add_square(last - 1)
+        res = stage.tile([PARTS, P], F32, name="res")
+        sq = stage.tile([PARTS, P], F32, name="sq")
+        mean = kept("mean", [1, P], F32)
+        for bank, cols in zip(banks, half_cols):
+            nc.scalar.activation(out=sq[:, cols], in_=bank[:, 0 : P // 2], func=ACT.Square)
+        for bank, cols in zip(banks, half_cols):
+            nc.scalar.copy(out=res[:, cols], in_=bank[:, 0 : P // 2])
+            nc.sync.dma_start(out=out_0[PARTS * last : PARTS * (last + 1), cols], in_=res[:, cols])
+        for cols in half_cols:
+            nc.vector.tensor_tensor(out=total[:, cols], in0=total[:, cols], in1=sq[:, cols], op=ALU.add)
+            bank = new_bank()
+            nc.tensor.matmul(bank[:, 0 : P // 2], lhsT=ones[:], rhs=total[:, cols], start=True, stop=True)
+            nc.vector.tensor_scalar(
+                out=mean[:, cols], in0=bank[0:1, 0 : P // 2], scalar1=1.0 / M, scalar2=None, op0=ALU.mult
+            )
+        nc.sync.dma_start(out=out_1.rearrange("(o c) -> o c", o=1), in_=mean[:])

@@ -179,23 +179,31 @@ def tile_ritz_residual_block_s12_kernel(
                     )
             slots_out(b == 0, grouped, b, bank)
 
-        def turn(words0, words1):
+        halves = {}
+
+        def split_words(key, raw):
+            words = stage.tile([PARTS, 4, 2, PARTS], F32, name="halves")
+            nc.vector.tensor_copy(
+                out=words[:].rearrange("p x u (c i) -> p x c u i", i=4),
+                in_=raw[:].rearrange("p a j -> p (a j)").bitcast(F32).rearrange("p (x c i u) -> p x c u i", x=4, i=4, u=2),
+            )
+            halves[key] = words
+
+        def turn(words, x0, x1):
             bank = new_bank()
             for u in range(2):
-                for a, words in enumerate((words0, words1)):
+                for a, x in enumerate((x0, x1)):
                     col = 2 * PARTS * u + PARTS * a
-                    nc.tensor.transpose(bank[:, col : col + PARTS], words[:, u : 2 * PARTS : 2], ident[:])
+                    nc.tensor.transpose(bank[:, col : col + PARTS], words[:, x, u, :], ident[:])
             return bank
 
         def kry_bank(G, g, half, grouped, on_vector):
-            words = kry[2 * G + half][:].bitcast(F32)
-            bank = turn(words[:, 0, 256 * g : 256 * (g + 1)], words[:, 1, 256 * g : 256 * (g + 1)])
+            bank = turn(halves[("kry", 2 * G + half)], g, J_PASSES + g)
             dst = grouped[:].bitcast(F32).rearrange("p (t w) -> p t w", t=4)[:, :, PARTS * half : PARTS * (half + 1)]
             copy_out(on_vector, dst.rearrange("p t (q r u) -> p t q r u", q=8, r=8), bank[:].rearrange("p (u q t r) -> p t q r u", u=2, q=8, t=4))
 
         def bv_bank(C, half, grouped, on_vector):
-            words = bv_raw[C][:].bitcast(F32)
-            bank = turn(words[:, 2 * half, :], words[:, 2 * half + 1, :])
+            bank = turn(halves[("bv", C)], 2 * half, 2 * half + 1)
             dst = grouped[:].bitcast(F32).rearrange("p (h n u) -> p h n u", h=2, u=2)
             copy_out(on_vector, dst[:, half], bank[:].rearrange("p (u n) -> p n u", u=2))
 
@@ -263,80 +271,86 @@ def tile_ritz_residual_block_s12_kernel(
             return bank
 
         total = kept("total", [PARTS, P], F32)
-        results = {}
-        squares = {}
+        half_cols = [slice(0, P // 2), slice(P // 2, P)]
 
-        def square(n):
-            if n == 0:
-                nc.scalar.activation(out=total[:], in_=results[n][:], func=ACT.Square)
-            else:
-                sq = stage.tile([PARTS, P], F32, name="sq")
-                nc.scalar.activation(out=sq[:], in_=results[n][:], func=ACT.Square)
-                squares[n] = sq
+        def add_square(sq, cols):
+            nc.vector.tensor_tensor(out=total[:, cols], in0=total[:, cols], in1=sq[:, cols], op=ALU.add)
 
-        def add_square(n):
-            if n > 0:
-                nc.vector.tensor_tensor(out=total[:], in0=total[:], in1=squares[n][:], op=ALU.add)
-
-        def resid_tile(n):
-            bank = resid_matmuls(n, slice(0, P))
+        def store_tile(n, bank, on_vector):
             res = stage.tile([PARTS, P], F32, name="res")
-            copy_out(n % 2 == 0, res[:], bank[:])
+            copy_out(on_vector, res[:], bank[:])
             nc.sync.dma_start(out=out_0[PARTS * n : PARTS * (n + 1), :], in_=res[:])
-            results[n] = res
+
+        def square_tile(n):
+            bank = resid_matmuls(n, slice(0, P))
+            sq = total if n == 0 else stage.tile([PARTS, P], F32, name="sq")
+            nc.scalar.activation(out=sq[:], in_=bank[:], func=ACT.Square)
             flush()
-            if n >= 1:
-                square(n - 1)
-            if n >= 2:
-                add_square(n - 2)
+            return bank, sq
+
+        def later(job, *args):
+            pending.append(lambda: job(*args))
+
+        def quantize_staged(key):
+            quantize(key, staged[key])
 
         sort_right(0)
-        pending.append(lambda: sort_right(1))
+        later(sort_right, 1)
         a_quad(0, 0)
-        pending.append(lambda: sort_right(2))
+        later(sort_right, 2)
+        later(split_words, ("kry", 0), kry[0])
+        later(split_words, ("kry", 1), kry[1])
         a_quad(1, 0)
-        kry_quad(0)
+        later(split_words, ("kry", 2), kry[2])
+        later(split_words, ("kry", 3), kry[3])
         a_quad(2, 0)
-        kry_quad(1)
-        pending.append(lambda: interleave("coef0", coef_raw[0], False))
+        kry_quad(0)
+        later(split_words, ("kry", 4), kry[4])
         a_quad(0, 1)
-        pending.append(lambda: quantize(("coef", 0), staged["coef0"]))
-        pending.append(lambda: interleave("coef1", coef_raw[1], False))
-        kry_quad(2)
-        pending.append(lambda: quantize(("coef", 1), staged["coef1"]))
+        later(split_words, ("kry", 5), kry[5])
+        kry_quad(1)
+        later(interleave, ("coef", 0), coef_raw[0], False)
         a_quad(1, 1)
-        pending.append(lambda: interleave("proj", proj_raw, True))
-        v_quad(0)
-        pending.append(lambda: quantize(("proj",), staged["proj"]))
-        bv_run([0, 1])
-        v_quad(1)
+        later(quantize_staged, ("coef", 0))
+        kry_quad(2)
+        later(interleave, ("coef", 1), coef_raw[1], False)
         a_quad(2, 1)
+        later(quantize_staged, ("coef", 1))
+        later(split_words, ("bv", 0), bv_raw[0])
+        later(split_words, ("bv", 1), bv_raw[1])
+        a_quad(0, 2)
+        later(split_words, ("bv", 2), bv_raw[2])
+        a_quad(1, 2)
+        v_quad(0)
+        bv_run([0, 1])
+        later(interleave, ("proj",), proj_raw, True)
+        v_quad(1)
+        later(quantize_staged, ("proj",))
         bv_run([2])
         v_quad(2)
-        a_quad(0, 2)
-        a_quad(1, 2)
-        for n in range(4):
-            resid_tile(n)
         a_quad(2, 2)
         last = ROW_TILES - 1
-        for n in range(4, last):
-            resid_tile(n)
+        for n in range(last - 1):
+            bank, sq = square_tile(n)
+            store_tile(n, bank, n % 2 == 0)
+            if n > 0:
+                add_square(sq, slice(0, P))
+        held_bank, sq = square_tile(last - 1)
+        for cols in half_cols:
+            add_square(sq, cols)
 
-        half_cols = [slice(0, P // 2), slice(P // 2, P)]
         banks = [resid_matmuls(last, cols) for cols in half_cols]
-        square(last - 1)
-        add_square(last - 2)
-        add_square(last - 1)
         res = stage.tile([PARTS, P], F32, name="res")
         sq = stage.tile([PARTS, P], F32, name="sq")
         mean = kept("mean", [1, P], F32)
         for bank, cols in zip(banks, half_cols):
             nc.scalar.activation(out=sq[:, cols], in_=bank[:, 0 : P // 2], func=ACT.Square)
+            add_square(sq, cols)
         for bank, cols in zip(banks, half_cols):
             nc.scalar.copy(out=res[:, cols], in_=bank[:, 0 : P // 2])
             nc.sync.dma_start(out=out_0[PARTS * last : PARTS * (last + 1), cols], in_=res[:, cols])
+        store_tile(last - 1, held_bank, True)
         for cols in half_cols:
-            nc.vector.tensor_tensor(out=total[:, cols], in0=total[:, cols], in1=sq[:, cols], op=ALU.add)
             bank = new_bank()
             nc.tensor.matmul(bank[:, 0 : P // 2], lhsT=ones[:], rhs=total[:, cols], start=True, stop=True)
             nc.vector.tensor_scalar(

@@ -19,11 +19,13 @@ ALU = mybir.AluOpType
 PARTS = 128
 PASS = 512
 BANK = 512
+HALF = BANK // 2
 M_PASSES = M // PASS
 K_PASSES = K // PASS
 J_PASSES = J // PASS
 ROW_TILES = M // PARTS
 WARM_UP = 7
+STAGED = 6
 
 
 def tile_ritz_residual_block_s12_kernel(
@@ -43,7 +45,7 @@ def tile_ritz_residual_block_s12_kernel(
             return psum.tile([PARTS, BANK], F32, name="bank")
 
         def new_grouped():
-            return stage.tile([PARTS, 4 * PASS], BF16, name="grouped", align_bytes=64, bufs=6)
+            return stage.tile([PARTS, 4 * PASS], BF16, name="grouped", align_bytes=64, bufs=STAGED)
 
         right_sc_raw = kept("right_sc_raw", [PARTS, K_PASSES, M], U8)
         left_sc = kept("left_sc", [PARTS, K_PASSES, M], U8)
@@ -61,9 +63,9 @@ def tile_ritz_residual_block_s12_kernel(
         for step in range(WARM_UP):
             nc.tensor.matmul(warm_bank[:], lhsT=warm[:, 0:PARTS], rhs=warm[:], start=True, stop=True)
 
-        def load_words(name, words, c):
-            tile = kept(name + str(c), [PARTS, K_PASSES, 2 * PASS], U8)
-            src = words[:, :, 2 * PASS * c : 2 * PASS * (c + 1)].rearrange("g p b -> p g b")
+        def load_words(name, words, chunk):
+            tile = kept(name + str(chunk), [PARTS, K_PASSES, 2 * PASS], U8)
+            src = words[:, :, 2 * PASS * chunk : 2 * PASS * (chunk + 1)].rearrange("g p b -> p g b")
             nc.sync.dma_start(out=tile[:].bitcast(I32), in_=src.bitcast(I32))
             return tile
 
@@ -89,15 +91,17 @@ def tile_ritz_residual_block_s12_kernel(
         load_scales(left_sc, left_scales)
         right_raw.append(load_words("right_raw", right_words, 1))
         right_raw.append(load_words("right_raw", right_words, 2))
-        kry = [load_rows("kry", krylov, 2 * i, 2) for i in range(2)]
-        left.append(load_words("left", left_words, 1))
-        kry.extend([load_rows("kry", krylov, 2 * i, 2) for i in range(2, 6)])
         coef_raw = [load_k_first("coef_raw", coef, g) for g in range(J_PASSES)]
+        left.append(load_words("left", left_words, 1))
+        kry = [load_rows("kry", krylov, 2 * i, 2) for i in range(ROW_TILES // 2)]
         left.append(load_words("left", left_words, 2))
-        bv_raw = [load_rows("bv_raw", bv, 4 * i, 4) for i in range(3)]
         proj_raw = load_k_first("proj_raw", proj, 0)
+        bv_raw = [load_rows("bv_raw", bv, 4 * i, 4) for i in range(M_PASSES)]
 
         mx = {}
+        staged = {}
+        right = {}
+        halves = {}
 
         def quantize(key, grouped):
             name = "_".join(str(part) for part in key)
@@ -106,13 +110,8 @@ def tile_ritz_residual_block_s12_kernel(
             nc.vector.quantize_mx(out=codes[:].bitcast(FP8X4), scales=scales[:], in_=grouped[:])
             mx[key] = (codes, scales)
 
-        def copy_out(on_vector, out, in_):
-            if on_vector:
-                nc.vector.tensor_copy(out=out, in_=in_)
-            else:
-                nc.scalar.copy(out=out, in_=in_)
-
-        right = {}
+        def quantize_staged(key):
+            quantize(key, staged[key])
 
         def sort_right(G):
             words = kept("right" + str(G), [PARTS, K_PASSES, 2 * PASS], U8)
@@ -127,8 +126,6 @@ def tile_ritz_residual_block_s12_kernel(
             )
             right[G] = (words, scales)
 
-        staged = {}
-
         def interleave(key, raw, negate):
             grouped = new_grouped()
             dst = grouped[:].rearrange("p (c i t) -> p c t i", i=4, t=4)
@@ -139,126 +136,133 @@ def tile_ritz_residual_block_s12_kernel(
                 nc.vector.tensor_copy(out=dst, in_=src)
             staged[key] = grouped
 
-        def slots_out(on_vector, grouped, b, bank):
-            copy_out(
-                on_vector,
-                grouped[:, BANK * b : BANK * (b + 1)].rearrange("p (n t) -> p n t", t=4),
-                bank[:].rearrange("p (t n) -> p n t", t=4),
-            )
-
-        def a_bank(G, C, b, grouped):
-            words, scales = right[G]
-            bank = new_bank()
-            for t in range(4):
-                for g in range(K_PASSES):
-                    nc.tensor.matmul_mx(
-                        out=bank[:, PARTS * t : PARTS * (t + 1)],
-                        lhsT=words[:, g, 2 * PARTS * t : 2 * PARTS * (t + 1)].bitcast(FP4X4),
-                        lhsT_scale=scales[:, g, PARTS * t : PARTS * (t + 1)],
-                        rhs=left[C][:, g, 2 * PARTS * b : 2 * PARTS * (b + 1)].bitcast(FP4X4),
-                        rhs_scale=left_sc[:, g, PASS * C + PARTS * b : PASS * C + PARTS * (b + 1)],
-                        start=(g == 0),
-                        stop=(g == K_PASSES - 1),
-                    )
-            slots_out(b == 0, grouped, b, bank)
-
-        def v_bank(G, b, grouped):
-            bank = new_bank()
-            for t in range(4):
-                for g in range(J_PASSES):
-                    k_codes, k_scales = mx[("kry", G, g)]
-                    c_codes, c_scales = mx[("coef", g)]
-                    nc.tensor.matmul_mx(
-                        out=bank[:, PARTS * t : PARTS * (t + 1)],
-                        lhsT=k_codes[:, PARTS * t : PARTS * (t + 1)].bitcast(FP8X4),
-                        lhsT_scale=k_scales[:, PARTS * t : PARTS * (t + 1)],
-                        rhs=c_codes[:, PARTS * b : PARTS * (b + 1)].bitcast(FP8X4),
-                        rhs_scale=c_scales[:, PARTS * b : PARTS * (b + 1)],
-                        start=(g == 0),
-                        stop=(g == J_PASSES - 1),
-                    )
-            slots_out(b == 0, grouped, b, bank)
-
-        halves = {}
-
         def split_words(key, raw):
-            words = stage.tile([PARTS, 4, 2, PARTS], F32, name="halves")
+            words = stage.tile([PARTS, 4, 2, PARTS], F32, name="halves", bufs=STAGED)
             nc.vector.tensor_copy(
                 out=words[:].rearrange("p x u (c i) -> p x c u i", i=4),
                 in_=raw[:].rearrange("p a j -> p (a j)").bitcast(F32).rearrange("p (x c i u) -> p x c u i", x=4, i=4, u=2),
             )
             halves[key] = words
 
-        def turn(words, x0, x1):
-            bank = new_bank()
-            for u in range(2):
-                for a, x in enumerate((x0, x1)):
-                    col = 2 * PARTS * u + PARTS * a
-                    nc.tensor.transpose(bank[:, col : col + PARTS], words[:, x, u, :], ident[:])
-            return bank
-
-        def kry_bank(G, g, half, grouped, on_vector):
-            bank = turn(halves[("kry", 2 * G + half)], g, J_PASSES + g)
-            dst = grouped[:].bitcast(F32).rearrange("p (t w) -> p t w", t=4)[:, :, PARTS * half : PARTS * (half + 1)]
-            copy_out(on_vector, dst.rearrange("p t (q r u) -> p t q r u", q=8, r=8), bank[:].rearrange("p (u q t r) -> p t q r u", u=2, q=8, t=4))
-
-        def bv_bank(C, half, grouped, on_vector):
-            bank = turn(halves[("bv", C)], 2 * half, 2 * half + 1)
-            dst = grouped[:].bitcast(F32).rearrange("p (h n u) -> p h n u", h=2, u=2)
-            copy_out(on_vector, dst[:, half], bank[:].rearrange("p (u n) -> p n u", u=2))
+        def merge_pairs(key, pairs):
+            grouped = new_grouped()
+            nc.vector.tensor_copy(
+                out=grouped[:].bitcast(F32).rearrange("p (n u) -> p n u", u=2),
+                in_=pairs[:].bitcast(F32).rearrange("p u n -> p n u"),
+            )
+            following.append(lambda: quantize(key, grouped))
 
         pending = []
+        following = []
+
+        def later(job, *args):
+            pending.append(lambda: job(*args))
 
         def flush():
             for job in pending:
                 job()
             pending.clear()
+            pending.extend(following)
+            following.clear()
 
-        def later_quantize(key, grouped):
-            pending.append(lambda: quantize(key, grouped))
+        def copy_out(on_vector, out, in_):
+            if on_vector:
+                nc.vector.tensor_copy(out=out, in_=in_)
+            else:
+                nc.scalar.copy(out=out, in_=in_)
 
-        def a_quad(G, C):
+        def a_step(G, C):
+            words, scales = right[G]
+            pairs = stage.tile([PARTS, 2, 2 * PASS], BF16, name="pairs", bufs=3)
+            for h in range(2):
+                for u in range(2):
+                    bank = new_bank()
+                    for e in range(2):
+                        t = 2 * u + e
+                        for g in range(K_PASSES):
+                            nc.tensor.matmul_mx(
+                                out=bank[:, HALF * e : HALF * (e + 1)],
+                                lhsT=words[:, g, 2 * PARTS * t : 2 * PARTS * (t + 1)].bitcast(FP4X4),
+                                lhsT_scale=scales[:, g, PARTS * t : PARTS * (t + 1)],
+                                rhs=left[C][:, g, 2 * HALF * h : 2 * HALF * (h + 1)].bitcast(FP4X4),
+                                rhs_scale=left_sc[:, g, PASS * C + HALF * h : PASS * C + HALF * (h + 1)],
+                                start=(g == 0),
+                                stop=(g == K_PASSES - 1),
+                            )
+                    nc.scalar.copy(
+                        out=pairs[:, u, 2 * HALF * h : 2 * HALF * (h + 1)].rearrange("p (n e) -> p n e", e=2),
+                        in_=bank[:].rearrange("p (e n) -> p n e", e=2),
+                    )
+                    if h == 0 and u == 0:
+                        flush()
+            later(merge_pairs, ("a", G, C), pairs)
+
+        def v_step(G):
             grouped = new_grouped()
             for b in range(4):
-                a_bank(G, C, b, grouped)
+                bank = new_bank()
+                for t in range(4):
+                    for g in range(J_PASSES):
+                        k_codes, k_scales = mx[("kry", G, g)]
+                        c_codes, c_scales = mx[("coef", g)]
+                        nc.tensor.matmul_mx(
+                            out=bank[:, PARTS * t : PARTS * (t + 1)],
+                            lhsT=k_codes[:, PARTS * t : PARTS * (t + 1)].bitcast(FP8X4),
+                            lhsT_scale=k_scales[:, PARTS * t : PARTS * (t + 1)],
+                            rhs=c_codes[:, PARTS * b : PARTS * (b + 1)].bitcast(FP8X4),
+                            rhs_scale=c_scales[:, PARTS * b : PARTS * (b + 1)],
+                            start=(g == 0),
+                            stop=(g == J_PASSES - 1),
+                        )
+                copy_out(
+                    b == 0,
+                    grouped[:, BANK * b : BANK * (b + 1)].rearrange("p (n t) -> p n t", t=4),
+                    bank[:].rearrange("p (t n) -> p n t", t=4),
+                )
                 if b == 0:
                     flush()
-            later_quantize(("a", G, C), grouped)
+            later(quantize, ("v", G), grouped)
 
-        def v_quad(G):
-            grouped = new_grouped()
-            for b in range(4):
-                v_bank(G, b, grouped)
-                if b == 0:
-                    flush()
-            later_quantize(("v", G), grouped)
+        def turn(words, x0, x1):
+            bank = new_bank()
+            for u in range(2):
+                for a, x in enumerate((x0, x1)):
+                    col = HALF * u + PARTS * a
+                    nc.tensor.transpose(bank[:, col : col + PARTS], words[:, x, u, :], ident[:])
+            return bank
 
-        def kry_quad(G):
+        def kry_step(G):
             for g in range(J_PASSES):
                 grouped = new_grouped()
-                for half in range(2):
-                    first = g == 0 and half == 0
-                    kry_bank(G, g, half, grouped, first)
-                    if first:
+                for h in range(2):
+                    bank = turn(halves[("kry", 2 * G + h)], g, J_PASSES + g)
+                    dst = grouped[:].bitcast(F32).rearrange("p (t w) -> p t w", t=4)[:, :, PARTS * h : PARTS * (h + 1)]
+                    nc.scalar.copy(
+                        out=dst.rearrange("p t (q r u) -> p t q r u", q=8, r=8),
+                        in_=bank[:].rearrange("p (u q t r) -> p t q r u", u=2, q=8, t=4),
+                    )
+                    if g == 0 and h == 0:
                         flush()
-                later_quantize(("kry", G, g), grouped)
+                later(quantize, ("kry", G, g), grouped)
 
-        def bv_run(chunks):
+        def bv_step(chunks):
             for C in chunks:
                 grouped = new_grouped()
-                for half in range(2):
-                    first = C == chunks[0] and half == 0
-                    bv_bank(C, half, grouped, first)
+                for h in range(2):
+                    first = C == chunks[0] and h == 0
+                    bank = turn(halves[("bv", C)], 2 * h, 2 * h + 1)
+                    dst = grouped[:].bitcast(F32).rearrange("p (h n u) -> p h n u", h=2, u=2)
+                    copy_out(first, dst[:, h], bank[:].rearrange("p (u n) -> p n u", u=2))
                     if first:
                         flush()
-                later_quantize(("bv", C), grouped)
+                later(quantize, ("bv", C), grouped)
 
         def resid_matmuls(n, cols):
             C, b = divmod(n, 4)
             rows = slice(PARTS * b, PARTS * (b + 1))
-            pairs = [(mx[("a", G, C)], mx[("v", G)]) for G in range(M_PASSES)] + [(mx[("bv", C)], mx[("proj",)])]
+            operands = [(mx[("a", G, C)], mx[("v", G)]) for G in range(M_PASSES)] + [(mx[("bv", C)], mx[("proj",)])]
             bank = new_bank()
-            for i, (lhs, rhs) in enumerate(pairs):
+            for i, (lhs, rhs) in enumerate(operands):
                 nc.tensor.matmul_mx(
                     out=bank[:, 0 : cols.stop - cols.start],
                     lhsT=lhs[0][:, rows].bitcast(FP8X4),
@@ -266,12 +270,12 @@ def tile_ritz_residual_block_s12_kernel(
                     rhs=rhs[0][:, cols].bitcast(FP8X4),
                     rhs_scale=rhs[1][:, cols],
                     start=(i == 0),
-                    stop=(i == len(pairs) - 1),
+                    stop=(i == len(operands) - 1),
                 )
             return bank
 
         total = kept("total", [PARTS, P], F32)
-        half_cols = [slice(0, P // 2), slice(P // 2, P)]
+        half_cols = [slice(0, HALF), slice(HALF, P)]
 
         def add_square(sq, cols):
             nc.vector.tensor_tensor(out=total[:, cols], in0=total[:, cols], in1=sq[:, cols], op=ALU.add)
@@ -288,72 +292,66 @@ def tile_ritz_residual_block_s12_kernel(
             flush()
             return bank, sq
 
-        def later(job, *args):
-            pending.append(lambda: job(*args))
-
-        def quantize_staged(key):
-            quantize(key, staged[key])
-
         sort_right(0)
         later(sort_right, 1)
-        a_quad(0, 0)
+        a_step(0, 0)
         later(sort_right, 2)
-        later(split_words, ("kry", 0), kry[0])
-        later(split_words, ("kry", 1), kry[1])
-        a_quad(1, 0)
-        later(split_words, ("kry", 2), kry[2])
-        later(split_words, ("kry", 3), kry[3])
-        a_quad(2, 0)
-        kry_quad(0)
-        later(split_words, ("kry", 4), kry[4])
-        a_quad(0, 1)
-        later(split_words, ("kry", 5), kry[5])
-        kry_quad(1)
         later(interleave, ("coef", 0), coef_raw[0], False)
-        a_quad(1, 1)
-        later(quantize_staged, ("coef", 0))
-        kry_quad(2)
+        a_step(1, 0)
         later(interleave, ("coef", 1), coef_raw[1], False)
-        a_quad(2, 1)
+        later(split_words, ("kry", 0), kry[0])
+        a_step(2, 0)
+        later(split_words, ("kry", 1), kry[1])
+        later(quantize_staged, ("coef", 0))
+        later(split_words, ("kry", 2), kry[2])
+        a_step(0, 1)
+        later(split_words, ("kry", 3), kry[3])
         later(quantize_staged, ("coef", 1))
+        a_step(1, 1)
+        later(split_words, ("kry", 4), kry[4])
+        kry_step(0)
+        later(split_words, ("kry", 5), kry[5])
+        a_step(2, 1)
+        kry_step(1)
+        a_step(0, 2)
+        kry_step(2)
         later(split_words, ("bv", 0), bv_raw[0])
-        later(split_words, ("bv", 1), bv_raw[1])
-        a_quad(0, 2)
-        later(split_words, ("bv", 2), bv_raw[2])
-        a_quad(1, 2)
-        v_quad(0)
-        bv_run([0, 1])
+        v_step(0)
         later(interleave, ("proj",), proj_raw, True)
-        v_quad(1)
+        v_step(1)
         later(quantize_staged, ("proj",))
-        bv_run([2])
-        v_quad(2)
-        a_quad(2, 2)
+        bv_step([0])
+        v_step(2)
+        later(split_words, ("bv", 1), bv_raw[1])
+        a_step(1, 2)
+        later(split_words, ("bv", 2), bv_raw[2])
+        a_step(2, 2)
+
         last = ROW_TILES - 1
         for n in range(last - 1):
+            if n == 1:
+                bv_step([1, 2])
             bank, sq = square_tile(n)
             store_tile(n, bank, n % 2 == 0)
             if n > 0:
                 add_square(sq, slice(0, P))
+
         held_bank, sq = square_tile(last - 1)
         for cols in half_cols:
             add_square(sq, cols)
-
         banks = [resid_matmuls(last, cols) for cols in half_cols]
         res = stage.tile([PARTS, P], F32, name="res")
         sq = stage.tile([PARTS, P], F32, name="sq")
         mean = kept("mean", [1, P], F32)
         for bank, cols in zip(banks, half_cols):
-            nc.scalar.activation(out=sq[:, cols], in_=bank[:, 0 : P // 2], func=ACT.Square)
+            nc.scalar.activation(out=sq[:, cols], in_=bank[:, 0:HALF], func=ACT.Square)
             add_square(sq, cols)
         for bank, cols in zip(banks, half_cols):
-            nc.scalar.copy(out=res[:, cols], in_=bank[:, 0 : P // 2])
+            nc.scalar.copy(out=res[:, cols], in_=bank[:, 0:HALF])
             nc.sync.dma_start(out=out_0[PARTS * last : PARTS * (last + 1), cols], in_=res[:, cols])
         store_tile(last - 1, held_bank, True)
         for cols in half_cols:
             bank = new_bank()
-            nc.tensor.matmul(bank[:, 0 : P // 2], lhsT=ones[:], rhs=total[:, cols], start=True, stop=True)
-            nc.vector.tensor_scalar(
-                out=mean[:, cols], in0=bank[0:1, 0 : P // 2], scalar1=1.0 / M, scalar2=None, op0=ALU.mult
-            )
+            nc.tensor.matmul(bank[:, 0:HALF], lhsT=ones[:], rhs=total[:, cols], start=True, stop=True)
+            nc.vector.tensor_scalar(out=mean[:, cols], in0=bank[0:1, 0:HALF], scalar1=1.0 / M, scalar2=None, op0=ALU.mult)
         nc.sync.dma_start(out=out_1.rearrange("(o c) -> o c", o=1), in_=mean[:])

@@ -24,7 +24,7 @@ M_PASSES = M // PASS
 K_PASSES = K // PASS
 J_PASSES = J // PASS
 ROW_TILES = M // PARTS
-WARM_UP = 7
+WARM_UP = 10
 STAGED = 6
 
 
@@ -152,15 +152,20 @@ def tile_ritz_residual_block_s12_kernel(
             )
             following.append(lambda: quantize(key, grouped))
 
+        urgent = []
         pending = []
         following = []
+
+        def soon(job, *args):
+            urgent.append(lambda: job(*args))
 
         def later(job, *args):
             pending.append(lambda: job(*args))
 
         def flush():
-            for job in pending:
+            for job in urgent + pending:
                 job()
+            urgent.clear()
             pending.clear()
             pending.extend(following)
             following.clear()
@@ -293,38 +298,38 @@ def tile_ritz_residual_block_s12_kernel(
             return bank, sq
 
         sort_right(0)
-        later(sort_right, 1)
+        soon(sort_right, 1)
         a_step(0, 0)
-        later(sort_right, 2)
+        soon(sort_right, 2)
         later(interleave, ("coef", 0), coef_raw[0], False)
         a_step(1, 0)
         later(interleave, ("coef", 1), coef_raw[1], False)
-        later(split_words, ("kry", 0), kry[0])
+        soon(split_words, ("kry", 0), kry[0])
         a_step(2, 0)
-        later(split_words, ("kry", 1), kry[1])
+        soon(split_words, ("kry", 1), kry[1])
         later(quantize_staged, ("coef", 0))
-        later(split_words, ("kry", 2), kry[2])
+        soon(split_words, ("kry", 2), kry[2])
         a_step(0, 1)
-        later(split_words, ("kry", 3), kry[3])
+        soon(split_words, ("kry", 3), kry[3])
         later(quantize_staged, ("coef", 1))
         a_step(1, 1)
-        later(split_words, ("kry", 4), kry[4])
+        soon(split_words, ("kry", 4), kry[4])
         kry_step(0)
-        later(split_words, ("kry", 5), kry[5])
+        soon(split_words, ("kry", 5), kry[5])
         a_step(2, 1)
         kry_step(1)
         a_step(0, 2)
         kry_step(2)
-        later(split_words, ("bv", 0), bv_raw[0])
+        soon(split_words, ("bv", 0), bv_raw[0])
         v_step(0)
         later(interleave, ("proj",), proj_raw, True)
         v_step(1)
         later(quantize_staged, ("proj",))
         bv_step([0])
         v_step(2)
-        later(split_words, ("bv", 1), bv_raw[1])
+        soon(split_words, ("bv", 1), bv_raw[1])
         a_step(1, 2)
-        later(split_words, ("bv", 2), bv_raw[2])
+        soon(split_words, ("bv", 2), bv_raw[2])
         a_step(2, 2)
 
         last = ROW_TILES - 1

from contextlib import ExitStack

import concourse.mybir as mybir
from concourse.masks import make_identity

M, K, J, P = 1536, 1024, 1024, 512
FLOPS = 2 * (M * M * K + M * J * P + M * M * P + M * P * P)

F32 = mybir.dt.float32
BF16 = mybir.dt.bfloat16
I32 = mybir.dt.int32
U32 = mybir.dt.uint32
U8 = mybir.dt.uint8
FP8X4 = mybir.dt.float8_e4m3fn_x4
FP4X4 = mybir.dt.float4_e2m1fn_x4
ACT = mybir.ActivationFunctionType
ALU = mybir.AluOpType

PARTS = 128
PASS = 512
BANK = 512
HALF = BANK // 2
M_PASSES = M // PASS
K_PASSES = K // PASS
J_PASSES = J // PASS
ROW_TILES = M // PARTS
WARM_UP = 10
STAGED = 6


def tile_ritz_residual_block_s12_kernel(
    tc, left_words, left_scales, right_words, right_scales, krylov, coef, bv, proj, out_0, out_1
):
    nc = tc.nc
    with ExitStack() as ctx:
        keep = ctx.enter_context(tc.tile_pool(name="keep", bufs=1))
        stage = ctx.enter_context(tc.tile_pool(name="stage", bufs=4))
        psum = ctx.enter_context(tc.psum_pool(name="psum", bufs=8))
        ctx.enter_context(tc.manual_schedule())

        def kept(name, shape, dtype):
            return keep.tile(shape, dtype, name=name, align_bytes=64)

        def new_bank():
            return psum.tile([PARTS, BANK], F32, name="bank")

        def new_grouped():
            return stage.tile([PARTS, 4 * PASS], BF16, name="grouped", align_bytes=64, bufs=STAGED)

        right_sc_raw = kept("right_sc_raw", [PARTS, K_PASSES, M], U8)
        left_sc = kept("left_sc", [PARTS, K_PASSES, M], U8)
        nc.vector.memset(right_sc_raw[:].bitcast(I32), 0)
        nc.vector.memset(left_sc[:].bitcast(I32), 0)
        warm = kept("warm", [PARTS, BANK], BF16)
        nc.gpsimd.memset(warm[:], 0.0)
        ident = kept("ident", [PARTS, PARTS], F32)
        make_identity(nc, ident[:])
        ones = kept("ones", [PARTS, PARTS], F32)
        nc.gpsimd.memset(ones[:], 1.0)
        table = kept("table", [PARTS, 1], F32)
        nc.scalar.activation(out=table[:], in_=warm[:, 0:1], func=ACT.Square)
        warm_bank = new_bank()
        for step in range(WARM_UP):
            nc.tensor.matmul(warm_bank[:], lhsT=warm[:, 0:PARTS], rhs=warm[:], start=True, stop=True)

        def load_words(name, words, chunk):
            tile = kept(name + str(chunk), [PARTS, K_PASSES, 2 * PASS], U8)
            src = words[:, :, 2 * PASS * chunk : 2 * PASS * (chunk + 1)].rearrange("g p b -> p g b")
            nc.sync.dma_start(out=tile[:].bitcast(I32), in_=src.bitcast(I32))
            return tile

        def load_scales(plane, scales):
            rows = scales.bitcast(I32).rearrange("g (Q r) w -> r Q g w", r=4)
            for r in range(4):
                nc.sync.dma_start(out=plane[r:PARTS:32, :, :].bitcast(I32), in_=rows[r])

        def load_rows(name, x, first, count):
            tile = kept(name + str(first), [PARTS, count, x.shape[1]], BF16)
            src = x[PARTS * first : PARTS * (first + count), :].rearrange("(a p) j -> p a j", p=PARTS)
            nc.sync.dma_start(out=tile[:], in_=src)
            return tile

        def load_k_first(name, x, g):
            tile = kept(name + str(g), [PARTS, 4, P], BF16)
            nc.sync.dma_start(out=tile[:], in_=x[PASS * g : PASS * (g + 1), :].rearrange("(p t) c -> p t c", t=4))
            return tile

        right_raw = [load_words("right_raw", right_words, 0)]
        left = [load_words("left", left_words, 0)]
        load_scales(right_sc_raw, right_scales)
        load_scales(left_sc, left_scales)
        right_raw.append(load_words("right_raw", right_words, 1))
        right_raw.append(load_words("right_raw", right_words, 2))
        coef_raw = [load_k_first("coef_raw", coef, g) for g in range(J_PASSES)]
        left.append(load_words("left", left_words, 1))
        kry = [load_rows("kry", krylov, 2 * i, 2) for i in range(ROW_TILES // 2)]
        left.append(load_words("left", left_words, 2))
        proj_raw = load_k_first("proj_raw", proj, 0)
        bv_raw = [load_rows("bv_raw", bv, 4 * i, 4) for i in range(M_PASSES)]

        mx = {}
        staged = {}
        right = {}
        halves = {}

        def quantize(key, grouped):
            name = "_".join(str(part) for part in key)
            codes = kept("codes_" + name, [PARTS, PASS], U32)
            scales = kept("scales_" + name, [PARTS, PASS], U8)
            nc.vector.quantize_mx(out=codes[:].bitcast(FP8X4), scales=scales[:], in_=grouped[:])
            mx[key] = (codes, scales)

        def quantize_staged(key):
            quantize(key, staged[key])

        def sort_right(G):
            words = kept("right" + str(G), [PARTS, K_PASSES, 2 * PASS], U8)
            scales = kept("right_sc" + str(G), [PARTS, K_PASSES, PASS], U8)
            nc.vector.tensor_copy(
                out=words[:].bitcast(I32).rearrange("p g (t q w) -> p g t q w", t=4, w=4),
                in_=right_raw[G][:].bitcast(I32).rearrange("p g (q t w) -> p g t q w", t=4, w=4),
            )
            nc.vector.tensor_copy(
                out=scales[:].bitcast(I32).rearrange("p g (t q w) -> p g t q w", t=4, w=2),
                in_=right_sc_raw[:, :, PASS * G : PASS * (G + 1)].bitcast(I32).rearrange("p g (q t w) -> p g t q w", t=4, w=2),
            )
            right[G] = (words, scales)

        def interleave(key, raw, negate):
            grouped = new_grouped()
            dst = grouped[:].rearrange("p (c i t) -> p c t i", i=4, t=4)
            src = raw[:].rearrange("p t (c i) -> p c t i", i=4)
            if negate:
                nc.vector.tensor_scalar(out=dst, in0=src, scalar1=-1.0, scalar2=None, op0=ALU.mult)
            else:
                nc.vector.tensor_copy(out=dst, in_=src)
            staged[key] = grouped

        def split_words(key, raw):
            words = stage.tile([PARTS, 4, 2, PARTS], F32, name="halves", bufs=STAGED)
            nc.vector.tensor_copy(
                out=words[:].rearrange("p x u (c i) -> p x c u i", i=4),
                in_=raw[:].rearrange("p a j -> p (a j)").bitcast(F32).rearrange("p (x c i u) -> p x c u i", x=4, i=4, u=2),
            )
            halves[key] = words

        def merge_pairs(key, pairs):
            grouped = new_grouped()
            nc.vector.tensor_copy(
                out=grouped[:].bitcast(F32).rearrange("p (n u) -> p n u", u=2),
                in_=pairs[:].bitcast(F32).rearrange("p u n -> p n u"),
            )
            following.append(lambda: quantize(key, grouped))

        urgent = []
        pending = []
        following = []

        def soon(job, *args):
            urgent.append(lambda: job(*args))

        def later(job, *args):
            pending.append(lambda: job(*args))

        def flush():
            for job in urgent + pending:
                job()
            urgent.clear()
            pending.clear()
            pending.extend(following)
            following.clear()

        def copy_out(on_vector, out, in_):
            if on_vector:
                nc.vector.tensor_copy(out=out, in_=in_)
            else:
                nc.scalar.copy(out=out, in_=in_)

        def a_step(G, C):
            words, scales = right[G]
            pairs = stage.tile([PARTS, 2, 2 * PASS], BF16, name="pairs", bufs=3)
            for h in range(2):
                for u in range(2):
                    bank = new_bank()
                    for e in range(2):
                        t = 2 * u + e
                        for g in range(K_PASSES):
                            nc.tensor.matmul_mx(
                                out=bank[:, HALF * e : HALF * (e + 1)],
                                lhsT=words[:, g, 2 * PARTS * t : 2 * PARTS * (t + 1)].bitcast(FP4X4),
                                lhsT_scale=scales[:, g, PARTS * t : PARTS * (t + 1)],
                                rhs=left[C][:, g, 2 * HALF * h : 2 * HALF * (h + 1)].bitcast(FP4X4),
                                rhs_scale=left_sc[:, g, PASS * C + HALF * h : PASS * C + HALF * (h + 1)],
                                start=(g == 0),
                                stop=(g == K_PASSES - 1),
                            )
                    nc.scalar.copy(
                        out=pairs[:, u, 2 * HALF * h : 2 * HALF * (h + 1)].rearrange("p (n e) -> p n e", e=2),
                        in_=bank[:].rearrange("p (e n) -> p n e", e=2),
                    )
                    if h == 0 and u == 0:
                        flush()
            later(merge_pairs, ("a", G, C), pairs)

        def v_step(G):
            grouped = new_grouped()
            for b in range(4):
                bank = new_bank()
                for t in range(4):
                    for g in range(J_PASSES):
                        k_codes, k_scales = mx[("kry", G, g)]
                        c_codes, c_scales = mx[("coef", g)]
                        nc.tensor.matmul_mx(
                            out=bank[:, PARTS * t : PARTS * (t + 1)],
                            lhsT=k_codes[:, PARTS * t : PARTS * (t + 1)].bitcast(FP8X4),
                            lhsT_scale=k_scales[:, PARTS * t : PARTS * (t + 1)],
                            rhs=c_codes[:, PARTS * b : PARTS * (b + 1)].bitcast(FP8X4),
                            rhs_scale=c_scales[:, PARTS * b : PARTS * (b + 1)],
                            start=(g == 0),
                            stop=(g == J_PASSES - 1),
                        )
                copy_out(
                    b == 0,
                    grouped[:, BANK * b : BANK * (b + 1)].rearrange("p (n t) -> p n t", t=4),
                    bank[:].rearrange("p (t n) -> p n t", t=4),
                )
                if b == 0:
                    flush()
            later(quantize, ("v", G), grouped)

        def turn(words, x0, x1):
            bank = new_bank()
            for u in range(2):
                for a, x in enumerate((x0, x1)):
                    col = HALF * u + PARTS * a
                    nc.tensor.transpose(bank[:, col : col + PARTS], words[:, x, u, :], ident[:])
            return bank

        def kry_step(G):
            for g in range(J_PASSES):
                grouped = new_grouped()
                for h in range(2):
                    bank = turn(halves[("kry", 2 * G + h)], g, J_PASSES + g)
                    dst = grouped[:].bitcast(F32).rearrange("p (t w) -> p t w", t=4)[:, :, PARTS * h : PARTS * (h + 1)]
                    nc.scalar.copy(
                        out=dst.rearrange("p t (q r u) -> p t q r u", q=8, r=8),
                        in_=bank[:].rearrange("p (u q t r) -> p t q r u", u=2, q=8, t=4),
                    )
                    if g == 0 and h == 0:
                        flush()
                later(quantize, ("kry", G, g), grouped)

        def bv_step(chunks):
            for C in chunks:
                grouped = new_grouped()
                for h in range(2):
                    first = C == chunks[0] and h == 0
                    bank = turn(halves[("bv", C)], 2 * h, 2 * h + 1)
                    dst = grouped[:].bitcast(F32).rearrange("p (h n u) -> p h n u", h=2, u=2)
                    copy_out(first, dst[:, h], bank[:].rearrange("p (u n) -> p n u", u=2))
                    if first:
                        flush()
                later(quantize, ("bv", C), grouped)

        def resid_matmuls(n, cols):
            C, b = divmod(n, 4)
            rows = slice(PARTS * b, PARTS * (b + 1))
            operands = [(mx[("a", G, C)], mx[("v", G)]) for G in range(M_PASSES)] + [(mx[("bv", C)], mx[("proj",)])]
            bank = new_bank()
            for i, (lhs, rhs) in enumerate(operands):
                nc.tensor.matmul_mx(
                    out=bank[:, 0 : cols.stop - cols.start],
                    lhsT=lhs[0][:, rows].bitcast(FP8X4),
                    lhsT_scale=lhs[1][:, rows],
                    rhs=rhs[0][:, cols].bitcast(FP8X4),
                    rhs_scale=rhs[1][:, cols],
                    start=(i == 0),
                    stop=(i == len(operands) - 1),
                )
            return bank

        total = kept("total", [PARTS, P], F32)
        half_cols = [slice(0, HALF), slice(HALF, P)]

        def add_square(sq, cols):
            nc.vector.tensor_tensor(out=total[:, cols], in0=total[:, cols], in1=sq[:, cols], op=ALU.add)

        def store_tile(n, bank, on_vector):
            res = stage.tile([PARTS, P], F32, name="res")
            copy_out(on_vector, res[:], bank[:])
            nc.sync.dma_start(out=out_0[PARTS * n : PARTS * (n + 1), :], in_=res[:])

        def square_tile(n):
            bank = resid_matmuls(n, slice(0, P))
            sq = total if n == 0 else stage.tile([PARTS, P], F32, name="sq")
            nc.scalar.activation(out=sq[:], in_=bank[:], func=ACT.Square)
            flush()
            return bank, sq

        sort_right(0)
        soon(sort_right, 1)
        a_step(0, 0)
        soon(sort_right, 2)
        later(interleave, ("coef", 0), coef_raw[0], False)
        a_step(1, 0)
        later(interleave, ("coef", 1), coef_raw[1], False)
        soon(split_words, ("kry", 0), kry[0])
        a_step(2, 0)
        soon(split_words, ("kry", 1), kry[1])
        later(quantize_staged, ("coef", 0))
        soon(split_words, ("kry", 2), kry[2])
        a_step(0, 1)
        soon(split_words, ("kry", 3), kry[3])
        later(quantize_staged, ("coef", 1))
        a_step(1, 1)
        soon(split_words, ("kry", 4), kry[4])
        kry_step(0)
        soon(split_words, ("kry", 5), kry[5])
        a_step(2, 1)
        kry_step(1)
        a_step(0, 2)
        kry_step(2)
        soon(split_words, ("bv", 0), bv_raw[0])
        v_step(0)
        later(interleave, ("proj",), proj_raw, True)
        v_step(1)
        later(quantize_staged, ("proj",))
        bv_step([0])
        v_step(2)
        soon(split_words, ("bv", 1), bv_raw[1])
        a_step(1, 2)
        soon(split_words, ("bv", 2), bv_raw[2])
        a_step(2, 2)

        last = ROW_TILES - 1
        for n in range(last - 1):
            if n == 1:
                bv_step([1, 2])
            bank, sq = square_tile(n)
            store_tile(n, bank, n % 2 == 0)
            if n > 0:
                add_square(sq, slice(0, P))

        held_bank, sq = square_tile(last - 1)
        for cols in half_cols:
            add_square(sq, cols)
        banks = [resid_matmuls(last, cols) for cols in half_cols]
        res = stage.tile([PARTS, P], F32, name="res")
        sq = stage.tile([PARTS, P], F32, name="sq")
        mean = kept("mean", [1, P], F32)
        for bank, cols in zip(banks, half_cols):
            nc.scalar.activation(out=sq[:, cols], in_=bank[:, 0:HALF], func=ACT.Square)
            add_square(sq, cols)
        for bank, cols in zip(banks, half_cols):
            nc.scalar.copy(out=res[:, cols], in_=bank[:, 0:HALF])
            nc.sync.dma_start(out=out_0[PARTS * last : PARTS * (last + 1), cols], in_=res[:, cols])
        store_tile(last - 1, held_bank, True)
        for cols in half_cols:
            bank = new_bank()
            nc.tensor.matmul(bank[:, 0:HALF], lhsT=ones[:], rhs=total[:, cols], start=True, stop=True)
            nc.vector.tensor_scalar(out=mean[:, cols], in0=bank[0:1, 0:HALF], scalar1=1.0 / M, scalar2=None, op0=ALU.mult)
        nc.sync.dma_start(out=out_1.rearrange("(o c) -> o c", o=1), in_=mean[:])
